import numpy as np
import ml_dtypes


def mxq(x, axis, fmt="e4m3"):
    dtype, down = {"e4m3": (ml_dtypes.float8_e4m3fn, 7), "e5m2": (ml_dtypes.float8_e5m2, 14)}[fmt]
    v = np.moveaxis(np.asarray(x, np.float32).astype(ml_dtypes.bfloat16).astype(np.float64), axis, -1)
    blocks = v.reshape(v.shape[:-1] + (-1, 32))
    amax = np.abs(blocks).max(-1, keepdims=True)
    byte = np.maximum(np.where(amax > 0, np.frexp(amax)[1] - 1 + 127, 0) - down, 1)
    scale = np.exp2(byte - 127.0)
    codes = (blocks / scale).astype(np.float32).astype(dtype).astype(np.float64)
    return np.moveaxis((codes * scale).reshape(v.shape), -1, axis)


WIDE = False


def mx_kscale(k):
    if not WIDE:
        return np.ones(k)
    levels = np.array([10, -10, 5, -5, 0])
    if k % 512:
        return np.exp2(np.random.permutation(np.resize(levels, k // 32))).repeat(32)
    a = np.empty((k // 512, 16))
    for p in range(k // 512):
        a[p, :8] = np.random.permutation(np.resize(levels, 8))
        for g in range(8):
            far = levels[np.abs(levels - a[p, g]) >= 10]
            a[p, g + 8] = far[np.random.randint(len(far))]
    return np.exp2(a.ravel()).repeat(32)


def f64(x):
    return np.asarray(x).astype(np.float64)


def striped8(idx):
    return np.concatenate([v.reshape(-1, 16).T for v in idx]).astype(np.uint16)


def unstriped8(offs):
    return np.stack([offs[16 * g:16 * g + 16].T.reshape(-1) for g in range(8)]).astype(np.int64)


E2M1 = np.array([0.0, 0.5, 1.0, 1.5, 2.0, 3.0, 4.0, 6.0, -0.0, -0.5, -1.0, -1.5, -2.0, -3.0, -4.0, -6.0])


def pack_weight(w, fmt):
    k, n = w.shape
    w = f64(np.asarray(w, np.float32).astype(ml_dtypes.bfloat16)).reshape(k // 32, 32, n)
    amax = np.abs(w).max(1)
    if fmt == "e4m3":
        byte = np.frexp(amax)[1] - 1 + 127 - 7
    else:
        mant, ex = np.frexp(amax / 6.0)
        byte = np.where(mant > 0.5, ex, ex - 1) + 127
    byte = np.clip(np.where(amax > 0, byte, 1), 1, 254)
    scaled = (w * np.exp2(127.0 - byte)[:, None, :]).reshape(k, n).astype(np.float32)
    by_word = np.ascontiguousarray(scaled.reshape(k // 512, 128, 4, n).transpose(0, 1, 3, 2))
    if fmt == "e4m3":
        words = by_word.astype(ml_dtypes.float8_e4m3fn).view(np.uint8)
    else:
        c = by_word.astype(ml_dtypes.float4_e2m1fn).view(np.uint8) & 0xF
        words = (c[..., 0::2] | (c[..., 1::2] << 4)).reshape(k // 512, 128, 2 * n)
    return np.ascontiguousarray(words), np.ascontiguousarray(byte.astype(np.uint8).reshape(k // 512, 16, n))


def unpack_weight(words, scales, fmt):
    g, _, n = scales.shape
    words = np.ascontiguousarray(words).reshape(g, 128, n, -1)
    if fmt == "e4m3":
        vals = words.view(ml_dtypes.float8_e4m3fn).astype(np.float64)
    else:
        nib = np.empty((g, 128, n, 4), np.uint8)
        nib[..., 0::2] = words & 0xF
        nib[..., 1::2] = words >> 4
        vals = E2M1[nib]
    vals = vals * np.repeat(np.exp2(scales.astype(np.float64) - 127.0), 8, axis=1)[..., None]
    return vals.transpose(0, 1, 3, 2).reshape(g * 512, n)


def gelu(v):
    return 0.5 * v * (1.0 + np.tanh(np.sqrt(2.0 / np.pi) * (v + 0.044715 * v**3)))


K, M, T, S = 512, 512, 1024, 512


def setup_inputs():
    n = np.random.standard_normal
    s = mx_kscale(K)[:, None]
    p_w = pack_weight(n((K, M)) / np.sqrt(K) / s, "e4m3")
    return {
        "x": (n((K, S)) * s).astype(np.float32),
        "w_words": p_w[0],
        "w_scales": p_w[1],
        "b": (0.3 * n(512)).astype(np.float32),
        "wgo": np.repeat(np.random.uniform(0.5, 2.0, (8, S)), 16, axis=0).astype(np.float32),
        "offs": striped8(np.stack([np.random.permutation(T)[:S] for _ in range(8)])),
    }


def reference(x, w_words, w_scales, b, wgo, offs):
    x_ = mxq(f64(x), 0, "e4m3")
    w_ = unpack_weight(w_words, w_scales, "e4m3")
    y = w_.T @ x_
    place = unstriped8(offs)[np.arange(M) % 128 // 16]
    out = np.zeros((M, T))
    out[np.arange(M)[:, None], place] = f64(wgo)[np.arange(M) % 128] * (gelu(y + f64(b)[:, None]))
    return out

@@ -1,0 +1,116 @@
+from contextlib import ExitStack
+
+import concourse.mybir as mybir
+
+K, M, T, S = 512, 512, 1024, 512
+FLOPS = 2 * K * M * S
+
+F32 = mybir.dt.float32
+BF16 = mybir.dt.bfloat16
+I32 = mybir.dt.int32
+U32 = mybir.dt.uint32
+U16 = mybir.dt.uint16
+U8 = mybir.dt.uint8
+FP8X4 = mybir.dt.float8_e4m3fn_x4
+ACT = mybir.ActivationFunctionType
+MULT = mybir.AluOpType.mult
+
+P = 128
+PACK = 4
+HALF = 256
+
+
+def tile_list_hscat_gelu_kernel(tc, x, w_words, w_scales, b, wgo, offs, out):
+    nc = tc.nc
+    with ExitStack() as ctx:
+        lists = ctx.enter_context(tc.tile_pool(name="lists", bufs=1))
+        keep = ctx.enter_context(tc.tile_pool(name="keep", bufs=1))
+        psum = ctx.enter_context(tc.psum_pool(name="psum", bufs=1))
+
+        offsets = lists.tile([P, S // 16], U16, name="offsets")
+        w_codes = keep.tile([P, M], U32, name="w_codes", align_bytes=64)
+        w_plane = keep.tile([P, M], U8, name="w_plane", align_bytes=64)
+        bias = keep.tile([P, M // P], F32, name="bias")
+        wgo_sb = [keep.tile([P, HALF], F32, name=f"wgo{h}") for h in range(2)]
+        raw = [keep.tile([P, PACK, HALF], F32, name=f"raw{h}", tag=f"raw{h}", align_bytes=64) for h in range(2)]
+        windows = [keep.tile([P, T], F32, name=f"window{m}") for m in range(4)]
+        dummy = keep.tile([P, 1], F32, name="dummy")
+
+        x_rows = x.rearrange("(p j) w -> p j w", j=PACK)
+        nc.gpsimd.memset(dummy[:], 0.0)
+        nc.sync.dma_start(raw[0][:], x_rows[:, :, 0:HALF])
+        nc.scalar.activation(dummy[:], dummy[:], ACT.Gelu_apprx_tanh)
+        nc.vector.memset(w_plane[:].bitcast(I32), 0)
+        for q in range(4):
+            nc.sync.dma_start(
+                w_plane[32 * q : 32 * q + 4, :].bitcast(I32), w_scales[0, 4 * q : 4 * q + 4, :].bitcast(I32)
+            )
+        nc.sync.dma_start(w_codes[:].bitcast(I32), w_words[0].rearrange("p n t -> p (n t)").bitcast(I32))
+        with nc.allow_non_contiguous_dma(reason="one bias a partition"):
+            nc.sync.dma_start(bias[:], b.rearrange("(m p) -> p m", p=P))
+        nc.sync.dma_start(offsets[:], offs)
+        nc.sync.dma_start(wgo_sb[0][:], wgo[:, 0:HALF])
+        nc.sync.dma_start(raw[1][:], x_rows[:, :, HALF:S])
+        nc.sync.dma_start(wgo_sb[1][:], wgo[:, HALF:S])
+        for m in range(3):
+            nc.vector.memset(windows[m][:].bitcast(I32), 0)
+        for m in range(3, 4):
+            for c in range(0, T, HALF):
+                nc.gpsimd.memset(windows[m][:, c : c + HALF], 0.0)
+
+        acc = [psum.tile([P, S], F32, name=f"acc{m}") for m in range(4)]
+        codes = [None, None]
+        planes = [None, None]
+        acts = {}
+
+        def quantize(h, split, tag_in, tag_out):
+            grouped = keep.tile([P, HALF, PACK], BF16, name=f"grouped{h}", tag=tag_in, align_bytes=64)
+            codes[h] = keep.tile([P, HALF], U32, name=f"codes{h}", tag=tag_out, align_bytes=64)
+            planes[h] = keep.tile([P, HALF], U8, name=f"plane{h}", align_bytes=64)
+            if split:
+                nc.vector.tensor_copy(grouped[:, 0:split, :], raw[h][:, :, 0:split].rearrange("p j w -> p w j"))
+            nc.scalar.copy(grouped[:, split:HALF, :], raw[h][:, :, split:HALF].rearrange("p j w -> p w j"))
+            nc.vector.quantize_mx(
+                out=codes[h][:].bitcast(FP8X4), scales=planes[h][:], in_=grouped[:].rearrange("p w j -> p (w j)")
+            )
+
+        def multiply(h, m):
+            cols = slice(P * m, P * (m + 1))
+            nc.tensor.matmul_mx(
+                out=acc[m][:, HALF * h : HALF * (h + 1)],
+                lhsT=w_codes[:, cols].bitcast(FP8X4),
+                lhsT_scale=w_plane[:, cols],
+                rhs=codes[h][:].bitcast(FP8X4),
+                rhs_scale=planes[h][:],
+                start=True,
+                stop=True,
+            )
+
+        def activate(h, m):
+            tag = {(0, 1): "late", (0, 2): "raw1"}.get((h, m), f"act{h}{m}")
+            act = keep.tile([P, HALF], F32, name=f"act{h}{m}", tag=tag, align_bytes=64)
+            nc.scalar.activation(
+                act[:], acc[m][:, HALF * h : HALF * (h + 1)], ACT.Gelu_apprx_tanh, bias=bias[:, m : m + 1]
+            )
+            acts[h, m] = act
+
+        def place(h, m):
+            nc.vector.tensor_tensor(
+                windows[m][:].indirect(offsets[:, 16 * h : 16 * (h + 1)]), acts[h, m][:], wgo_sb[h][:], MULT
+            )
+
+        quantize(0, 168, "grouped0", "share")
+        for m in range(4):
+            multiply(0, m)
+        for m in range(2):
+            activate(0, m)
+            place(0, m)
+        quantize(1, 0, "share", "late")
+        for m in range(2, 4):
+            activate(0, m)
+            place(0, m)
+        for m in range(4):
+            multiply(1, m)
+            activate(1, m)
+            place(1, m)
+            nc.sync.dma_start(out[P * m : P * (m + 1), :], windows[m][:])

@@ -17,7 +17,7 @@ MULT = mybir.AluOpType.mult
 
 P = 128
 PACK = 4
-HALF = 256
+PIECES = [(0, 128), (128, 256), (256, 512)]
 
 
 def tile_list_hscat_gelu_kernel(tc, x, w_words, w_scales, b, wgo, offs, out):
@@ -31,53 +31,59 @@ def tile_list_hscat_gelu_kernel(tc, x, w_words, w_scales, b, wgo, offs, out):
         w_codes = keep.tile([P, M], U32, name="w_codes", align_bytes=64)
         w_plane = keep.tile([P, M], U8, name="w_plane", align_bytes=64)
         bias = keep.tile([P, M // P], F32, name="bias")
-        wgo_sb = [keep.tile([P, HALF], F32, name=f"wgo{h}") for h in range(2)]
-        raw = [keep.tile([P, PACK, HALF], F32, name=f"raw{h}", tag=f"raw{h}", align_bytes=64) for h in range(2)]
-        windows = [keep.tile([P, T], F32, name=f"window{m}") for m in range(4)]
+        wgo_sb = [keep.tile([P, 256], F32, name=f"wgo{h}") for h in range(2)]
+        raw = [keep.tile([P, PACK, hi - lo], F32, name=f"raw{h}", tag=f"raw{h}", align_bytes=64) for h, (lo, hi) in enumerate(PIECES)]
+        windows = {}
         dummy = keep.tile([P, 1], F32, name="dummy")
 
         x_rows = x.rearrange("(p j) w -> p j w", j=PACK)
-        nc.gpsimd.memset(dummy[:], 0.0)
-        nc.sync.dma_start(raw[0][:], x_rows[:, :, 0:HALF])
+        nc.gpsimd.dma_start(wgo_sb[0][:], wgo[:, 0:256])
+        nc.vector.memset(dummy[:], 0.0)
+        nc.sync.dma_start(raw[0][:], x_rows[:, :, 0:128])
         nc.scalar.activation(dummy[:], dummy[:], ACT.Gelu_apprx_tanh)
-        nc.vector.memset(w_plane[:].bitcast(I32), 0)
+        nc.sync.dma_start(w_codes[:].bitcast(I32), w_words[0].rearrange("p n t -> p (n t)").bitcast(I32))
         for q in range(4):
             nc.sync.dma_start(
                 w_plane[32 * q : 32 * q + 4, :].bitcast(I32), w_scales[0, 4 * q : 4 * q + 4, :].bitcast(I32)
             )
-        nc.sync.dma_start(w_codes[:].bitcast(I32), w_words[0].rearrange("p n t -> p (n t)").bitcast(I32))
         with nc.allow_non_contiguous_dma(reason="one bias a partition"):
             nc.sync.dma_start(bias[:], b.rearrange("(m p) -> p m", p=P))
         nc.sync.dma_start(offsets[:], offs)
-        nc.sync.dma_start(wgo_sb[0][:], wgo[:, 0:HALF])
-        nc.sync.dma_start(raw[1][:], x_rows[:, :, HALF:S])
-        nc.sync.dma_start(wgo_sb[1][:], wgo[:, HALF:S])
-        for m in range(3):
-            nc.vector.memset(windows[m][:].bitcast(I32), 0)
-        for m in range(3, 4):
-            for c in range(0, T, HALF):
-                nc.gpsimd.memset(windows[m][:, c : c + HALF], 0.0)
+        nc.sync.dma_start(raw[1][:], x_rows[:, :, 128:256])
+        nc.sync.dma_start(raw[2][:], x_rows[:, :, 256:512])
+        nc.sync.dma_start(wgo_sb[1][:], wgo[:, 256:512])
+
+        def clear(m, engine, tag):
+            windows[m] = keep.tile([P, T], F32, name=f"window{m}", tag=tag, align_bytes=64)
+            engine.memset(windows[m][:].bitcast(I32), 0)
+
+        clear(0, nc.vector, "window0")
+        clear(1, nc.vector, "window1")
 
         acc = [psum.tile([P, S], F32, name=f"acc{m}") for m in range(4)]
-        codes = [None, None]
-        planes = [None, None]
+        codes = {}
+        planes = {}
         acts = {}
 
-        def quantize(h, split, tag_in, tag_out):
-            grouped = keep.tile([P, HALF, PACK], BF16, name=f"grouped{h}", tag=tag_in, align_bytes=64)
-            codes[h] = keep.tile([P, HALF], U32, name=f"codes{h}", tag=tag_out, align_bytes=64)
-            planes[h] = keep.tile([P, HALF], U8, name=f"plane{h}", align_bytes=64)
+        def quantize(h, split):
+            lo, hi = PIECES[h]
+            n = hi - lo
+            grouped = keep.tile([P, n, PACK], BF16, name=f"grouped{h}", tag={1: "codes0"}.get(h, f"grouped{h}"), align_bytes=64)
+            codes[h] = keep.tile([P, n], U32, name=f"codes{h}", tag=f"codes{h}", align_bytes=64)
+            planes[h] = keep.tile([P, n], U8, name=f"plane{h}", tag=f"plane{h}", align_bytes=64)
             if split:
                 nc.vector.tensor_copy(grouped[:, 0:split, :], raw[h][:, :, 0:split].rearrange("p j w -> p w j"))
-            nc.scalar.copy(grouped[:, split:HALF, :], raw[h][:, :, split:HALF].rearrange("p j w -> p w j"))
+            if split < n:
+                nc.scalar.copy(grouped[:, split:n, :], raw[h][:, :, split:n].rearrange("p j w -> p w j"))
             nc.vector.quantize_mx(
                 out=codes[h][:].bitcast(FP8X4), scales=planes[h][:], in_=grouped[:].rearrange("p w j -> p (w j)")
             )
 
         def multiply(h, m):
+            lo, hi = PIECES[h]
             cols = slice(P * m, P * (m + 1))
             nc.tensor.matmul_mx(
-                out=acc[m][:, HALF * h : HALF * (h + 1)],
+                out=acc[m][:, lo:hi],
                 lhsT=w_codes[:, cols].bitcast(FP8X4),
                 lhsT_scale=w_plane[:, cols],
                 rhs=codes[h][:].bitcast(FP8X4),
@@ -87,30 +93,33 @@ def tile_list_hscat_gelu_kernel(tc, x, w_words, w_scales, b, wgo, offs, out):
             )
 
         def activate(h, m):
-            tag = {(0, 1): "late", (0, 2): "raw1"}.get((h, m), f"act{h}{m}")
-            act = keep.tile([P, HALF], F32, name=f"act{h}{m}", tag=tag, align_bytes=64)
-            nc.scalar.activation(
-                act[:], acc[m][:, HALF * h : HALF * (h + 1)], ACT.Gelu_apprx_tanh, bias=bias[:, m : m + 1]
-            )
+            lo, hi = PIECES[h]
+            act = keep.tile([P, hi - lo], F32, name=f"act{h}{m}", tag={(0, 2): "raw1", (1, 2): "raw2"}.get((h, m), f"act{h}{m}"), align_bytes=64)
+            nc.scalar.activation(act[:], acc[m][:, lo:hi], ACT.Gelu_apprx_tanh, bias=bias[:, m : m + 1])
             acts[h, m] = act
 
         def place(h, m):
+            lo, hi = PIECES[h]
             nc.vector.tensor_tensor(
-                windows[m][:].indirect(offsets[:, 16 * h : 16 * (h + 1)]), acts[h, m][:], wgo_sb[h][:], MULT
+                windows[m][:].indirect(offsets[:, lo // 16 : hi // 16]),
+                acts[h, m][:],
+                wgo_sb[lo // 256][:, lo % 256 : lo % 256 + hi - lo],
+                MULT,
             )
 
-        quantize(0, 168, "grouped0", "share")
+        quantize(0, 80)
         for m in range(4):
             multiply(0, m)
-        for m in range(2):
-            activate(0, m)
-            place(0, m)
-        quantize(1, 0, "share", "late")
-        for m in range(2, 4):
-            activate(0, m)
-            place(0, m)
-        for m in range(4):
-            multiply(1, m)
-            activate(1, m)
-            place(1, m)
-            nc.sync.dma_start(out[P * m : P * (m + 1), :], windows[m][:])
+        clear(2, nc.gpsimd, "grouped0")
+        clear(3, nc.gpsimd, "plane0")
+        for h in range(3):
+            for m in range(4):
+                if m == 2 and h < 2:
+                    quantize(h + 1, 0)
+                activate(h, m)
+                place(h, m)
+                if h == 2:
+                    nc.sync.dma_start(out[P * m : P * (m + 1), :], windows[m][:])
+            if h < 2:
+                for m in range(4):
+                    multiply(h + 1, m)

@@ -30,25 +30,32 @@ def tile_list_hscat_gelu_kernel(tc, x, w_words, w_scales, b, wgo, offs, out):
         offsets = lists.tile([P, S // 16], U16, name="offsets")
         w_codes = keep.tile([P, M], U32, name="w_codes", align_bytes=64)
         w_plane = keep.tile([P, M], U8, name="w_plane", align_bytes=64)
-        bias = keep.tile([P, M // P], F32, name="bias")
+        bias_rows = keep.tile([P, P], F32, name="bias_rows", align_bytes=64)
+        bias = keep.tile([P, P], F32, name="bias", align_bytes=64)
         wgo_sb = [keep.tile([P, 256], F32, name=f"wgo{h}") for h in range(2)]
         raw = [keep.tile([P, PACK, hi - lo], F32, name=f"raw{h}", tag=f"raw{h}", align_bytes=64) for h, (lo, hi) in enumerate(PIECES)]
         windows = {}
         dummy = keep.tile([P, 1], F32, name="dummy")
 
         x_rows = x.rearrange("(p j) w -> p j w", j=PACK)
-        nc.gpsimd.dma_start(wgo_sb[0][:], wgo[:, 0:256])
-        nc.vector.memset(dummy[:], 0.0)
-        nc.sync.dma_start(raw[0][:], x_rows[:, :, 0:128])
-        nc.scalar.activation(dummy[:], dummy[:], ACT.Gelu_apprx_tanh)
-        nc.sync.dma_start(w_codes[:].bitcast(I32), w_words[0].rearrange("p n t -> p (n t)").bitcast(I32))
-        for q in range(4):
-            nc.sync.dma_start(
+
+        def load_scales(q, engine):
+            engine.dma_start(
                 w_plane[32 * q : 32 * q + 4, :].bitcast(I32), w_scales[0, 4 * q : 4 * q + 4, :].bitcast(I32)
             )
-        with nc.allow_non_contiguous_dma(reason="one bias a partition"):
-            nc.sync.dma_start(bias[:], b.rearrange("(m p) -> p m", p=P))
+
         nc.sync.dma_start(offsets[:], offs)
+        nc.sync.dma_start(raw[0][:], x_rows[:, :, 0:128])
+        nc.vector.memset(dummy[:], 0.0)
+        nc.vector.memset(bias_rows[:], 0.0)
+        nc.scalar.activation(dummy[:], dummy[:], ACT.Gelu_apprx_tanh)
+        for q in range(4):
+            load_scales(q, nc.sync)
+        nc.sync.dma_start(w_codes[:].bitcast(I32), w_words[0].rearrange("p n t -> p (n t)").bitcast(I32))
+        nc.sync.dma_start(
+            bias_rows[0:P:32, :].rearrange("q (m i) -> q m i", i=32), b.rearrange("(m q i) -> q m i", q=4, i=32)
+        )
+        nc.sync.dma_start(wgo_sb[0][:], wgo[:, 0:256])
         nc.sync.dma_start(raw[1][:], x_rows[:, :, 128:256])
         nc.sync.dma_start(raw[2][:], x_rows[:, :, 256:512])
         nc.sync.dma_start(wgo_sb[1][:], wgo[:, 256:512])
@@ -95,7 +102,7 @@ def tile_list_hscat_gelu_kernel(tc, x, w_words, w_scales, b, wgo, offs, out):
         def activate(h, m):
             lo, hi = PIECES[h]
             act = keep.tile([P, hi - lo], F32, name=f"act{h}{m}", tag={(0, 2): "raw1", (1, 2): "raw2"}.get((h, m), f"act{h}{m}"), align_bytes=64)
-            nc.scalar.activation(act[:], acc[m][:, lo:hi], ACT.Gelu_apprx_tanh, bias=bias[:, m : m + 1])
+            nc.scalar.activation(act[:], acc[m][:, lo:hi], ACT.Gelu_apprx_tanh, bias=bias[:, 32 * m : 32 * m + 1])
             acts[h, m] = act
 
         def place(h, m):
@@ -108,6 +115,7 @@ def tile_list_hscat_gelu_kernel(tc, x, w_words, w_scales, b, wgo, offs, out):
             )
 
         quantize(0, 80)
+        nc.vector.transpose(bias[:], bias_rows[:])
         for m in range(4):
             multiply(0, m)
         clear(2, nc.gpsimd, "grouped0")

@@ -18,6 +18,7 @@ MULT = mybir.AluOpType.mult
 P = 128
 PACK = 4
 PIECES = [(0, 128), (128, 256), (256, 512)]
+SPANS = PIECES + [(0, 512), (128, 512)]
 
 
 def tile_list_hscat_gelu_kernel(tc, x, w_words, w_scales, b, wgo, offs, out):
@@ -30,9 +31,8 @@ def tile_list_hscat_gelu_kernel(tc, x, w_words, w_scales, b, wgo, offs, out):
         offsets = lists.tile([P, S // 16], U16, name="offsets")
         w_codes = keep.tile([P, M], U32, name="w_codes", align_bytes=64)
         w_plane = keep.tile([P, M], U8, name="w_plane", align_bytes=64)
-        bias_rows = keep.tile([P, P], F32, name="bias_rows", align_bytes=64)
-        bias = keep.tile([P, P], F32, name="bias", align_bytes=64)
-        wgo_sb = [keep.tile([P, 256], F32, name=f"wgo{h}") for h in range(2)]
+        bias = keep.tile([P, M // P], F32, name="bias")
+        wgo_sb = keep.tile([P, S], F32, name="wgo_sb")
         raw = [keep.tile([P, PACK, hi - lo], F32, name=f"raw{h}", tag=f"raw{h}", align_bytes=64) for h, (lo, hi) in enumerate(PIECES)]
         windows = {}
         dummy = keep.tile([P, 1], F32, name="dummy")
@@ -47,18 +47,16 @@ def tile_list_hscat_gelu_kernel(tc, x, w_words, w_scales, b, wgo, offs, out):
         nc.sync.dma_start(offsets[:], offs)
         nc.sync.dma_start(raw[0][:], x_rows[:, :, 0:128])
         nc.vector.memset(dummy[:], 0.0)
-        nc.vector.memset(bias_rows[:], 0.0)
         nc.scalar.activation(dummy[:], dummy[:], ACT.Gelu_apprx_tanh)
         for q in range(4):
             load_scales(q, nc.sync)
         nc.sync.dma_start(w_codes[:].bitcast(I32), w_words[0].rearrange("p n t -> p (n t)").bitcast(I32))
-        nc.sync.dma_start(
-            bias_rows[0:P:32, :].rearrange("q (m i) -> q m i", i=32), b.rearrange("(m q i) -> q m i", q=4, i=32)
-        )
-        nc.sync.dma_start(wgo_sb[0][:], wgo[:, 0:256])
+        with nc.allow_non_contiguous_dma(reason="one bias a partition"):
+            nc.sync.dma_start(bias[:], b.rearrange("(m p) -> p m", p=P))
+        nc.sync.dma_start(wgo_sb[:, 0:256], wgo[:, 0:256])
         nc.sync.dma_start(raw[1][:], x_rows[:, :, 128:256])
         nc.sync.dma_start(raw[2][:], x_rows[:, :, 256:512])
-        nc.sync.dma_start(wgo_sb[1][:], wgo[:, 256:512])
+        nc.sync.dma_start(wgo_sb[:, 256:512], wgo[:, 256:512])
 
         def clear(m, engine, tag):
             windows[m] = keep.tile([P, T], F32, name=f"window{m}", tag=tag, align_bytes=64)
@@ -66,6 +64,7 @@ def tile_list_hscat_gelu_kernel(tc, x, w_words, w_scales, b, wgo, offs, out):
 
         clear(0, nc.vector, "window0")
         clear(1, nc.vector, "window1")
+        clear(2, nc.vector, "window2")
 
         acc = [psum.tile([P, S], F32, name=f"acc{m}") for m in range(4)]
         codes = {}
@@ -100,34 +99,43 @@ def tile_list_hscat_gelu_kernel(tc, x, w_words, w_scales, b, wgo, offs, out):
             )
 
         def activate(h, m):
-            lo, hi = PIECES[h]
-            act = keep.tile([P, hi - lo], F32, name=f"act{h}{m}", tag={(0, 2): "raw1", (1, 2): "raw2"}.get((h, m), f"act{h}{m}"), align_bytes=64)
-            nc.scalar.activation(act[:], acc[m][:, lo:hi], ACT.Gelu_apprx_tanh, bias=bias[:, 32 * m : 32 * m + 1])
+            lo, hi = SPANS[h]
+            act = keep.tile([P, hi - lo], F32, name=f"act{h}{m}", tag={(0, 2): "raw1", (1, 0): "raw2"}.get((h, m), f"act{h}{m}"), align_bytes=64)
+            nc.scalar.activation(act[:], acc[m][:, lo:hi], ACT.Gelu_apprx_tanh, bias=bias[:, m : m + 1])
             acts[h, m] = act
 
         def place(h, m):
-            lo, hi = PIECES[h]
+            lo, hi = SPANS[h]
             nc.vector.tensor_tensor(
                 windows[m][:].indirect(offsets[:, lo // 16 : hi // 16]),
                 acts[h, m][:],
-                wgo_sb[lo // 256][:, lo % 256 : lo % 256 + hi - lo],
+                wgo_sb[:, lo:hi],
                 MULT,
             )
 
         quantize(0, 80)
-        nc.vector.transpose(bias[:], bias_rows[:])
         for m in range(4):
             multiply(0, m)
-        clear(2, nc.gpsimd, "grouped0")
-        clear(3, nc.gpsimd, "plane0")
-        for h in range(3):
-            for m in range(4):
-                if m == 2 and h < 2:
-                    quantize(h + 1, 0)
-                activate(h, m)
-                place(h, m)
-                if h == 2:
-                    nc.sync.dma_start(out[P * m : P * (m + 1), :], windows[m][:])
-            if h < 2:
-                for m in range(4):
-                    multiply(h + 1, m)
+        clear(3, nc.vector, "raw0")
+        def finish(h, m):
+            activate(h, m)
+            place(h, m)
+
+        def store(m):
+            nc.sync.dma_start(out[P * m : P * (m + 1), :], windows[m][:])
+
+        finish(0, 0)
+        finish(0, 1)
+        quantize(1, 0)
+        finish(0, 2)
+        finish(0, 3)
+        for m in range(4):
+            multiply(1, m)
+        quantize(2, 0)
+        finish(1, 0)
+        finish(1, 1)
+        for m in range(4):
+            multiply(2, m)
+        for h, m in ((2, 0), (2, 1), (4, 2), (4, 3)):
+            finish(h, m)
+            store(m)

@@ -53,10 +53,10 @@ def tile_list_hscat_gelu_kernel(tc, x, w_words, w_scales, b, wgo, offs, out):
         nc.sync.dma_start(w_codes[:].bitcast(I32), w_words[0].rearrange("p n t -> p (n t)").bitcast(I32))
         with nc.allow_non_contiguous_dma(reason="one bias a partition"):
             nc.sync.dma_start(bias[:], b.rearrange("(m p) -> p m", p=P))
-        nc.sync.dma_start(wgo_sb[:, 0:256], wgo[:, 0:256])
+        nc.sync.dma_start(wgo_sb[:, 0:128], wgo[:, 0:128])
         nc.sync.dma_start(raw[1][:], x_rows[:, :, 128:256])
         nc.sync.dma_start(raw[2][:], x_rows[:, :, 256:512])
-        nc.sync.dma_start(wgo_sb[:, 256:512], wgo[:, 256:512])
+        nc.sync.dma_start(wgo_sb[:, 128:512], wgo[:, 128:512])
 
         def clear(m, engine, tag):
             windows[m] = keep.tile([P, T], F32, name=f"window{m}", tag=tag, align_bytes=64)
@@ -78,9 +78,15 @@ def tile_list_hscat_gelu_kernel(tc, x, w_words, w_scales, b, wgo, offs, out):
             codes[h] = keep.tile([P, n], U32, name=f"codes{h}", tag=f"codes{h}", align_bytes=64)
             planes[h] = keep.tile([P, n], U8, name=f"plane{h}", tag=f"plane{h}", align_bytes=64)
             if split:
-                nc.vector.tensor_copy(grouped[:, 0:split, :], raw[h][:, :, 0:split].rearrange("p j w -> p w j"))
+                nc.vector.tensor_copy(
+                    grouped[:, 0:split, :].rearrange("p (c i) t -> p c t i", i=4),
+                    raw[h][:, :, 0:split].rearrange("p t (c i) -> p c t i", i=4),
+                )
             if split < n:
-                nc.scalar.copy(grouped[:, split:n, :], raw[h][:, :, split:n].rearrange("p j w -> p w j"))
+                nc.scalar.copy(
+                    grouped[:, split:n, :].rearrange("p (c i) t -> p c t i", i=4),
+                    raw[h][:, :, split:n].rearrange("p t (c i) -> p c t i", i=4),
+                )
             nc.vector.quantize_mx(
                 out=codes[h][:].bitcast(FP8X4), scales=planes[h][:], in_=grouped[:].rearrange("p w j -> p (w j)")
             )
@@ -113,7 +119,7 @@ def tile_list_hscat_gelu_kernel(tc, x, w_words, w_scales, b, wgo, offs, out):
                 MULT,
             )
 
-        quantize(0, 80)
+        quantize(0, 128)
         for m in range(4):
             multiply(0, m)
         clear(3, nc.vector, "raw0")

@@ -64,7 +64,6 @@ def tile_list_hscat_gelu_kernel(tc, x, w_words, w_scales, b, wgo, offs, out):
 
         clear(0, nc.vector, "window0")
         clear(1, nc.vector, "window1")
-        clear(2, nc.vector, "window2")
 
         acc = [psum.tile([P, S], F32, name=f"acc{m}") for m in range(4)]
         codes = {}
@@ -122,7 +121,8 @@ def tile_list_hscat_gelu_kernel(tc, x, w_words, w_scales, b, wgo, offs, out):
         quantize(0, 128)
         for m in range(4):
             multiply(0, m)
-        clear(3, nc.vector, "raw0")
+        clear(2, nc.vector, "raw0")
+        clear(3, nc.gpsimd, "plane0")
         def finish(h, m):
             activate(h, m)
             place(h, m)

@@ -118,11 +118,34 @@ def tile_list_hscat_gelu_kernel(tc, x, w_words, w_scales, b, wgo, offs, out):
                 MULT,
             )
 
-        quantize(0, 128)
-        for m in range(4):
+        codes[0] = keep.tile([P, 128], U32, name="codes0", tag="codes0", align_bytes=64)
+        planes[0] = keep.tile([P, 128], U8, name="plane0", tag="plane0", align_bytes=64)
+        first = keep.tile([P, 128, PACK], BF16, name="grouped0", tag="grouped0", align_bytes=64)
+        for lo in (0, 64):
+            nc.vector.tensor_copy(
+                first[:, lo : lo + 64, :].rearrange("p (c i) t -> p c t i", i=4),
+                raw[0][:, :, lo : lo + 64].rearrange("p t (c i) -> p c t i", i=4),
+            )
+        lead = [psum.tile([P, 64], F32, name=f"lead{u}") for u in range(2)]
+        for u, lo in enumerate((0, 64)):
+            nc.vector.quantize_mx(
+                out=codes[0][:, lo : lo + 64].bitcast(FP8X4),
+                scales=planes[0][:, lo : lo + 64],
+                in_=first[:, lo : lo + 64, :].rearrange("p w j -> p (w j)"),
+            )
+            nc.tensor.matmul_mx(
+                out=lead[u][:],
+                lhsT=w_codes[:, 0:P].bitcast(FP8X4),
+                lhsT_scale=w_plane[:, 0:P],
+                rhs=codes[0][:, lo : lo + 64].bitcast(FP8X4),
+                rhs_scale=planes[0][:, lo : lo + 64],
+                start=True,
+                stop=True,
+            )
+        for m in range(1, 4):
             multiply(0, m)
-        clear(2, nc.vector, "raw0")
-        clear(3, nc.gpsimd, "plane0")
+        clear(3, nc.gpsimd, "grouped0")
+        clear(2, nc.gpsimd, "plane0")
         def finish(h, m):
             activate(h, m)
             place(h, m)
@@ -130,7 +153,10 @@ def tile_list_hscat_gelu_kernel(tc, x, w_words, w_scales, b, wgo, offs, out):
         def store(m):
             nc.sync.dma_start(out[P * m : P * (m + 1), :], windows[m][:])
 
-        finish(0, 0)
+        acts[0, 0] = keep.tile([P, 128], F32, name="act00", align_bytes=64)
+        for u, lo in enumerate((0, 64)):
+            nc.scalar.activation(acts[0, 0][:, lo : lo + 64], lead[u][:], ACT.Gelu_apprx_tanh, bias=bias[:, 0:1])
+        place(0, 0)
         finish(0, 1)
         quantize(1, 0)
         finish(0, 2)

@@ -12,13 +12,16 @@ U32 = mybir.dt.uint32
 U16 = mybir.dt.uint16
 U8 = mybir.dt.uint8
 FP8X4 = mybir.dt.float8_e4m3fn_x4
-ACT = mybir.ActivationFunctionType
+GELU = mybir.ActivationFunctionType.Gelu_apprx_tanh
 MULT = mybir.AluOpType.mult
 
 P = 128
 PACK = 4
+GROUP = 16
+ROW_TILES = M // P
 PIECES = [(0, 128), (128, 256), (256, 512)]
-SPANS = PIECES + [(0, 512), (128, 512)]
+FIRST = PIECES[0][1]
+HALF = FIRST // 2
 
 
 def tile_list_hscat_gelu_kernel(tc, x, w_words, w_scales, b, wgo, offs, out):
@@ -28,146 +31,132 @@ def tile_list_hscat_gelu_kernel(tc, x, w_words, w_scales, b, wgo, offs, out):
         keep = ctx.enter_context(tc.tile_pool(name="keep", bufs=1))
         psum = ctx.enter_context(tc.psum_pool(name="psum", bufs=1))
 
-        offsets = lists.tile([P, S // 16], U16, name="offsets")
+        offsets = lists.tile([P, S // GROUP], U16, name="offsets")
         w_codes = keep.tile([P, M], U32, name="w_codes", align_bytes=64)
-        w_plane = keep.tile([P, M], U8, name="w_plane", align_bytes=64)
-        bias = keep.tile([P, M // P], F32, name="bias")
+        w_scale = keep.tile([P, M], U8, name="w_scale", align_bytes=64)
+        bias = keep.tile([P, ROW_TILES], F32, name="bias")
         wgo_sb = keep.tile([P, S], F32, name="wgo_sb")
-        raw = [keep.tile([P, PACK, hi - lo], F32, name=f"raw{h}", tag=f"raw{h}", align_bytes=64) for h, (lo, hi) in enumerate(PIECES)]
-        windows = {}
-        dummy = keep.tile([P, 1], F32, name="dummy")
+        raw = [
+            keep.tile([P, PACK, hi - lo], F32, name=f"raw{h}", tag=f"raw{h}", align_bytes=64)
+            for h, (lo, hi) in enumerate(PIECES)
+        ]
+        warm = keep.tile([P, 1], F32, name="warm")
 
-        x_rows = x.rearrange("(p j) w -> p j w", j=PACK)
-
-        def load_scales(q, engine):
-            engine.dma_start(
-                w_plane[32 * q : 32 * q + 4, :].bitcast(I32), w_scales[0, 4 * q : 4 * q + 4, :].bitcast(I32)
-            )
-
+        x_rows = x.rearrange("(p t) c -> p t c", t=PACK)
         nc.sync.dma_start(offsets[:], offs)
-        nc.sync.dma_start(raw[0][:], x_rows[:, :, 0:128])
-        nc.vector.memset(dummy[:], 0.0)
-        nc.scalar.activation(dummy[:], dummy[:], ACT.Gelu_apprx_tanh)
+        nc.sync.dma_start(raw[0][:], x_rows[:, :, 0:FIRST])
+        nc.vector.memset(warm[:], 0.0)
+        nc.scalar.activation(warm[:], warm[:], GELU)
         for q in range(4):
-            load_scales(q, nc.sync)
+            nc.sync.dma_start(
+                w_scale[32 * q : 32 * q + 4, :].bitcast(I32), w_scales[0, 4 * q : 4 * q + 4, :].bitcast(I32)
+            )
         nc.sync.dma_start(w_codes[:].bitcast(I32), w_words[0].rearrange("p n t -> p (n t)").bitcast(I32))
-        with nc.allow_non_contiguous_dma(reason="one bias a partition"):
+        with nc.allow_non_contiguous_dma(reason="one bias value a partition"):
             nc.sync.dma_start(bias[:], b.rearrange("(m p) -> p m", p=P))
-        nc.sync.dma_start(wgo_sb[:, 0:128], wgo[:, 0:128])
-        nc.sync.dma_start(raw[1][:], x_rows[:, :, 128:256])
-        nc.sync.dma_start(raw[2][:], x_rows[:, :, 256:512])
-        nc.sync.dma_start(wgo_sb[:, 128:512], wgo[:, 128:512])
+        nc.sync.dma_start(wgo_sb[:, 0:FIRST], wgo[:, 0:FIRST])
+        for h in (1, 2):
+            lo, hi = PIECES[h]
+            nc.sync.dma_start(raw[h][:], x_rows[:, :, lo:hi])
+        nc.sync.dma_start(wgo_sb[:, FIRST:S], wgo[:, FIRST:S])
+
+        windows = {}
 
         def clear(m, engine, tag):
             windows[m] = keep.tile([P, T], F32, name=f"window{m}", tag=tag, align_bytes=64)
             engine.memset(windows[m][:].bitcast(I32), 0)
 
+        rounded, x_codes, x_scale = {}, {}, {}
+
+        def make_piece_tiles(h, rounded_tag):
+            width = PIECES[h][1] - PIECES[h][0]
+            rounded[h] = keep.tile([P, width, PACK], BF16, name=f"rounded{h}", tag=rounded_tag, align_bytes=64)
+            x_codes[h] = keep.tile([P, width], U32, name=f"x_codes{h}", tag=f"x_codes{h}", align_bytes=64)
+            x_scale[h] = keep.tile([P, width], U8, name=f"x_scale{h}", tag=f"x_scale{h}", align_bytes=64)
+
+        def round_columns(h, cols, copy):
+            copy(
+                rounded[h][:, cols, :].rearrange("p (c i) t -> p c t i", i=4),
+                raw[h][:, :, cols].rearrange("p t (c i) -> p c t i", i=4),
+            )
+
+        def quantize(h, cols):
+            nc.vector.quantize_mx(
+                out=x_codes[h][:, cols].bitcast(FP8X4),
+                scales=x_scale[h][:, cols],
+                in_=rounded[h][:, cols, :].rearrange("p c t -> p (c t)"),
+            )
+
+        def multiply(m, h, cols, sums):
+            rows = slice(P * m, P * (m + 1))
+            nc.tensor.matmul_mx(
+                out=sums,
+                lhsT=w_codes[:, rows].bitcast(FP8X4),
+                lhsT_scale=w_scale[:, rows],
+                rhs=x_codes[h][:, cols].bitcast(FP8X4),
+                rhs_scale=x_scale[h][:, cols],
+                start=True,
+                stop=True,
+            )
+
+        def multiply_piece(m, h):
+            lo, hi = PIECES[h]
+            multiply(m, h, slice(0, hi - lo), acc[m][:, lo:hi])
+
+        def gelu(m, result, sums):
+            nc.scalar.activation(result, sums, GELU, bias=bias[:, m : m + 1])
+
+        def place(m, lo, hi, values):
+            listed = windows[m][:].indirect(offsets[:, lo // GROUP : hi // GROUP])
+            nc.vector.tensor_tensor(listed, values, wgo_sb[:, lo:hi], MULT)
+
+        def finish(m, lo, hi, tag):
+            values = keep.tile([P, hi - lo], F32, name=f"values{m}_{lo}", tag=tag, align_bytes=64)
+            gelu(m, values[:], acc[m][:, lo:hi])
+            place(m, lo, hi, values[:])
+
         clear(0, nc.vector, "window0")
         clear(1, nc.vector, "window1")
 
-        acc = [psum.tile([P, S], F32, name=f"acc{m}") for m in range(4)]
-        codes = {}
-        planes = {}
-        acts = {}
+        acc = [psum.tile([P, S], F32, name=f"acc{m}") for m in range(ROW_TILES)]
 
-        def quantize(h, split):
-            lo, hi = PIECES[h]
-            n = hi - lo
-            grouped = keep.tile([P, n, PACK], BF16, name=f"grouped{h}", tag={1: "codes0"}.get(h, f"grouped{h}"), align_bytes=64)
-            codes[h] = keep.tile([P, n], U32, name=f"codes{h}", tag=f"codes{h}", align_bytes=64)
-            planes[h] = keep.tile([P, n], U8, name=f"plane{h}", tag=f"plane{h}", align_bytes=64)
-            if split:
-                nc.vector.tensor_copy(
-                    grouped[:, 0:split, :].rearrange("p (c i) t -> p c t i", i=4),
-                    raw[h][:, :, 0:split].rearrange("p t (c i) -> p c t i", i=4),
-                )
-            if split < n:
-                nc.scalar.copy(
-                    grouped[:, split:n, :].rearrange("p (c i) t -> p c t i", i=4),
-                    raw[h][:, :, split:n].rearrange("p t (c i) -> p c t i", i=4),
-                )
-            nc.vector.quantize_mx(
-                out=codes[h][:].bitcast(FP8X4), scales=planes[h][:], in_=grouped[:].rearrange("p w j -> p (w j)")
-            )
+        halves = [slice(0, HALF), slice(HALF, FIRST)]
+        make_piece_tiles(0, "rounded0")
+        round_columns(0, halves[0], nc.vector.tensor_copy)
+        round_columns(0, halves[1], nc.scalar.copy)
+        lead = [psum.tile([P, HALF], F32, name=f"lead{u}") for u in range(2)]
+        for cols, sums in zip(halves, lead):
+            quantize(0, cols)
+            multiply(0, 0, cols, sums[:])
+        for m in range(1, ROW_TILES):
+            multiply_piece(m, 0)
+        clear(3, nc.gpsimd, "rounded0")
+        clear(2, nc.gpsimd, "x_scale0")
 
-        def multiply(h, m):
-            lo, hi = PIECES[h]
-            cols = slice(P * m, P * (m + 1))
-            nc.tensor.matmul_mx(
-                out=acc[m][:, lo:hi],
-                lhsT=w_codes[:, cols].bitcast(FP8X4),
-                lhsT_scale=w_plane[:, cols],
-                rhs=codes[h][:].bitcast(FP8X4),
-                rhs_scale=planes[h][:],
-                start=True,
-                stop=True,
-            )
+        lead_values = keep.tile([P, FIRST], F32, name="lead_values", align_bytes=64)
+        for cols, sums in zip(halves, lead):
+            gelu(0, lead_values[:, cols], sums[:])
+        place(0, 0, FIRST, lead_values[:])
+        finish(1, 0, FIRST, "values1a")
 
-        def activate(h, m):
-            lo, hi = SPANS[h]
-            act = keep.tile([P, hi - lo], F32, name=f"act{h}{m}", tag={(0, 2): "raw1", (1, 0): "raw2"}.get((h, m), f"act{h}{m}"), align_bytes=64)
-            nc.scalar.activation(act[:], acc[m][:, lo:hi], ACT.Gelu_apprx_tanh, bias=bias[:, m : m + 1])
-            acts[h, m] = act
+        whole = [slice(0, hi - lo) for lo, hi in PIECES]
+        make_piece_tiles(1, "x_codes0")
+        round_columns(1, whole[1], nc.scalar.copy)
+        quantize(1, whole[1])
+        finish(2, 0, FIRST, "raw1")
+        finish(3, 0, FIRST, "values3a")
+        for m in range(ROW_TILES):
+            multiply_piece(m, 1)
 
-        def place(h, m):
-            lo, hi = SPANS[h]
-            nc.vector.tensor_tensor(
-                windows[m][:].indirect(offsets[:, lo // 16 : hi // 16]),
-                acts[h, m][:],
-                wgo_sb[:, lo:hi],
-                MULT,
-            )
+        make_piece_tiles(2, "rounded2")
+        round_columns(2, whole[2], nc.scalar.copy)
+        quantize(2, whole[2])
+        finish(0, *PIECES[1], "raw2")
+        finish(1, *PIECES[1], "values1b")
+        for m in range(ROW_TILES):
+            multiply_piece(m, 2)
 
-        codes[0] = keep.tile([P, 128], U32, name="codes0", tag="codes0", align_bytes=64)
-        planes[0] = keep.tile([P, 128], U8, name="plane0", tag="plane0", align_bytes=64)
-        first = keep.tile([P, 128, PACK], BF16, name="grouped0", tag="grouped0", align_bytes=64)
-        for lo in (0, 64):
-            nc.vector.tensor_copy(
-                first[:, lo : lo + 64, :].rearrange("p (c i) t -> p c t i", i=4),
-                raw[0][:, :, lo : lo + 64].rearrange("p t (c i) -> p c t i", i=4),
-            )
-        lead = [psum.tile([P, 64], F32, name=f"lead{u}") for u in range(2)]
-        for u, lo in enumerate((0, 64)):
-            nc.vector.quantize_mx(
-                out=codes[0][:, lo : lo + 64].bitcast(FP8X4),
-                scales=planes[0][:, lo : lo + 64],
-                in_=first[:, lo : lo + 64, :].rearrange("p w j -> p (w j)"),
-            )
-            nc.tensor.matmul_mx(
-                out=lead[u][:],
-                lhsT=w_codes[:, 0:P].bitcast(FP8X4),
-                lhsT_scale=w_plane[:, 0:P],
-                rhs=codes[0][:, lo : lo + 64].bitcast(FP8X4),
-                rhs_scale=planes[0][:, lo : lo + 64],
-                start=True,
-                stop=True,
-            )
-        for m in range(1, 4):
-            multiply(0, m)
-        clear(3, nc.gpsimd, "grouped0")
-        clear(2, nc.gpsimd, "plane0")
-        def finish(h, m):
-            activate(h, m)
-            place(h, m)
-
-        def store(m):
+        for m in range(ROW_TILES):
+            lo = PIECES[2][0] if m < 2 else PIECES[1][0]
+            finish(m, lo, S, f"values{m}c")
             nc.sync.dma_start(out[P * m : P * (m + 1), :], windows[m][:])
-
-        acts[0, 0] = keep.tile([P, 128], F32, name="act00", align_bytes=64)
-        for u, lo in enumerate((0, 64)):
-            nc.scalar.activation(acts[0, 0][:, lo : lo + 64], lead[u][:], ACT.Gelu_apprx_tanh, bias=bias[:, 0:1])
-        place(0, 0)
-        finish(0, 1)
-        quantize(1, 0)
-        finish(0, 2)
-        finish(0, 3)
-        for m in range(4):
-            multiply(1, m)
-        quantize(2, 0)
-        finish(1, 0)
-        finish(1, 1)
-        for m in range(4):
-            multiply(2, m)
-        for h, m in ((2, 0), (2, 1), (4, 2), (4, 3)):
-            finish(h, m)
-            store(m)

@@ -43,18 +43,22 @@ def tile_list_hscat_gelu_kernel(tc, x, w_words, w_scales, b, wgo, offs, out):
         warm = keep.tile([P, 1], F32, name="warm")
 
         x_rows = x.rearrange("(p t) c -> p t c", t=PACK)
-        nc.sync.dma_start(offsets[:], offs)
+        def load_scale(q, queue):
+            queue.dma_start(
+                w_scale[32 * q : 32 * q + 4, :].bitcast(I32), w_scales[0, 4 * q : 4 * q + 4, :].bitcast(I32)
+            )
+
+        load_scale(0, nc.scalar)
         nc.sync.dma_start(raw[0][:], x_rows[:, :, 0:FIRST])
         nc.vector.memset(warm[:], 0.0)
         nc.scalar.activation(warm[:], warm[:], GELU)
-        for q in range(4):
-            nc.sync.dma_start(
-                w_scale[32 * q : 32 * q + 4, :].bitcast(I32), w_scales[0, 4 * q : 4 * q + 4, :].bitcast(I32)
-            )
+        for q in (1, 2, 3):
+            load_scale(q, nc.sync)
         nc.sync.dma_start(w_codes[:].bitcast(I32), w_words[0].rearrange("p n t -> p (n t)").bitcast(I32))
         with nc.allow_non_contiguous_dma(reason="one bias value a partition"):
             nc.sync.dma_start(bias[:], b.rearrange("(m p) -> p m", p=P))
         nc.sync.dma_start(wgo_sb[:, 0:FIRST], wgo[:, 0:FIRST])
+        nc.sync.dma_start(offsets[:], offs)
         for h in (1, 2):
             lo, hi = PIECES[h]
             nc.sync.dma_start(raw[h][:], x_rows[:, :, lo:hi])

@@ -20,6 +20,7 @@ PACK = 4
 GROUP = 16
 ROW_TILES = M // P
 PIECES = [(0, 128), (128, 256), (256, 512)]
+LOADS = [(0, 128), (128, 320), (320, 512)]
 FIRST = PIECES[0][1]
 HALF = FIRST // 2
 
@@ -38,7 +39,7 @@ def tile_list_hscat_gelu_kernel(tc, x, w_words, w_scales, b, wgo, offs, out):
         wgo_sb = keep.tile([P, S], F32, name="wgo_sb")
         raw = [
             keep.tile([P, PACK, hi - lo], F32, name=f"raw{h}", tag=f"raw{h}", align_bytes=64)
-            for h, (lo, hi) in enumerate(PIECES)
+            for h, (lo, hi) in enumerate(LOADS)
         ]
         warm = keep.tile([P, 1], F32, name="warm")
 
@@ -60,7 +61,7 @@ def tile_list_hscat_gelu_kernel(tc, x, w_words, w_scales, b, wgo, offs, out):
         nc.sync.dma_start(wgo_sb[:, 0:FIRST], wgo[:, 0:FIRST])
         nc.sync.dma_start(offsets[:], offs)
         for h in (1, 2):
-            lo, hi = PIECES[h]
+            lo, hi = LOADS[h]
             nc.sync.dma_start(raw[h][:], x_rows[:, :, lo:hi])
         nc.sync.dma_start(wgo_sb[:, FIRST:S], wgo[:, FIRST:S])
 
@@ -78,10 +79,10 @@ def tile_list_hscat_gelu_kernel(tc, x, w_words, w_scales, b, wgo, offs, out):
             x_codes[h] = keep.tile([P, width], U32, name=f"x_codes{h}", tag=f"x_codes{h}", align_bytes=64)
             x_scale[h] = keep.tile([P, width], U8, name=f"x_scale{h}", tag=f"x_scale{h}", align_bytes=64)
 
-        def round_columns(h, cols, copy):
+        def round_columns(h, cols, copy, load=None, load_cols=None):
             copy(
                 rounded[h][:, cols, :].rearrange("p (c i) t -> p c t i", i=4),
-                raw[h][:, :, cols].rearrange("p t (c i) -> p c t i", i=4),
+                raw[h if load is None else load][:, :, load_cols or cols].rearrange("p t (c i) -> p c t i", i=4),
             )
 
         def quantize(h, cols):
@@ -147,13 +148,15 @@ def tile_list_hscat_gelu_kernel(tc, x, w_words, w_scales, b, wgo, offs, out):
         make_piece_tiles(1, "x_codes0")
         round_columns(1, whole[1], nc.scalar.copy)
         quantize(1, whole[1])
-        finish(2, 0, FIRST, "raw1")
+        gelu(2, raw[1][:, 0, 0:FIRST], acc[2][:, 0:FIRST])
+        place(2, 0, FIRST, raw[1][:, 0, 0:FIRST])
         finish(3, 0, FIRST, "values3a")
+        make_piece_tiles(2, "rounded2")
+        round_columns(2, slice(0, 64), nc.scalar.copy, 1, slice(128, 192))
         for m in range(ROW_TILES):
             multiply_piece(m, 1)
 
-        make_piece_tiles(2, "rounded2")
-        round_columns(2, whole[2], nc.scalar.copy)
+        round_columns(2, slice(64, 256), nc.scalar.copy, 2, slice(0, 192))
         quantize(2, whole[2])
         finish(0, *PIECES[1], "raw2")
         finish(1, *PIECES[1], "values1b")

@@ -158,12 +158,13 @@ def tile_list_hscat_gelu_kernel(tc, x, w_words, w_scales, b, wgo, offs, out):
 
         round_columns(2, slice(64, 256), nc.scalar.copy, 2, slice(0, 192))
         quantize(2, whole[2])
-        finish(0, *PIECES[1], "raw2")
-        finish(1, *PIECES[1], "values1b")
+        for m in range(ROW_TILES):
+            lo, hi = PIECES[1]
+            gelu(m, raw[2][:, m, 0 : hi - lo], acc[m][:, lo:hi])
+            place(m, lo, hi, raw[2][:, m, 0 : hi - lo])
         for m in range(ROW_TILES):
             multiply_piece(m, 2)
 
         for m in range(ROW_TILES):
-            lo = PIECES[2][0] if m < 2 else PIECES[1][0]
-            finish(m, lo, S, f"values{m}c")
+            finish(m, *PIECES[2], f"values{m}c")
             nc.sync.dma_start(out[P * m : P * (m + 1), :], windows[m][:])

@@ -20,8 +20,9 @@ PACK = 4
 GROUP = 16
 ROW_TILES = M // P
 PIECES = [(0, 128), (128, 256), (256, 512)]
-LOADS = [(0, 128), (128, 320), (320, 512)]
+LOADS = PIECES
 FIRST = PIECES[0][1]
+LEAD = 16
 HALF = FIRST // 2
 
 
@@ -37,10 +38,12 @@ def tile_list_hscat_gelu_kernel(tc, x, w_words, w_scales, b, wgo, offs, out):
         w_scale = keep.tile([P, M], U8, name="w_scale", align_bytes=64)
         bias = keep.tile([P, ROW_TILES], F32, name="bias")
         wgo_sb = keep.tile([P, S], F32, name="wgo_sb")
-        raw = [
-            keep.tile([P, PACK, hi - lo], F32, name=f"raw{h}", tag=f"raw{h}", align_bytes=64)
+        room = [0, FIRST - LEAD, 0]
+        flat = [
+            keep.tile([P, room[h] + PACK * (hi - lo)], F32, name=f"raw{h}", tag=f"raw{h}", align_bytes=64)
             for h, (lo, hi) in enumerate(LOADS)
         ]
+        raw = [flat[h][:, room[h] :].rearrange("p (t c) -> p t c", t=PACK) for h in range(len(LOADS))]
         warm = keep.tile([P, 1], F32, name="warm")
 
         x_rows = x.rearrange("(p t) c -> p t c", t=PACK)
@@ -50,7 +53,7 @@ def tile_list_hscat_gelu_kernel(tc, x, w_words, w_scales, b, wgo, offs, out):
             )
 
         load_scale(0, nc.scalar)
-        nc.sync.dma_start(raw[0][:], x_rows[:, :, 0:FIRST])
+        nc.sync.dma_start(raw[0], x_rows[:, :, 0:FIRST])
         nc.vector.memset(warm[:], 0.0)
         nc.scalar.activation(warm[:], warm[:], GELU)
         for q in (1, 2, 3):
@@ -62,7 +65,7 @@ def tile_list_hscat_gelu_kernel(tc, x, w_words, w_scales, b, wgo, offs, out):
         nc.sync.dma_start(offsets[:], offs)
         for h in (1, 2):
             lo, hi = LOADS[h]
-            nc.sync.dma_start(raw[h][:], x_rows[:, :, lo:hi])
+            nc.sync.dma_start(raw[h], x_rows[:, :, lo:hi])
         nc.sync.dma_start(wgo_sb[:, FIRST:S], wgo[:, FIRST:S])
 
         windows = {}
@@ -135,8 +138,8 @@ def tile_list_hscat_gelu_kernel(tc, x, w_words, w_scales, b, wgo, offs, out):
             multiply(0, 0, cols, sums[:])
         for m in range(1, ROW_TILES):
             multiply_piece(m, 0)
-        clear(3, nc.gpsimd, "rounded0")
-        clear(2, nc.gpsimd, "x_scale0")
+        clear(2, nc.gpsimd, "rounded0")
+        clear(3, nc.gpsimd, "x_scale0")
 
         lead_values = keep.tile([P, FIRST], F32, name="lead_values", align_bytes=64)
         for cols, sums in zip(halves, lead):
@@ -146,20 +149,22 @@ def tile_list_hscat_gelu_kernel(tc, x, w_words, w_scales, b, wgo, offs, out):
 
         whole = [slice(0, hi - lo) for lo, hi in PIECES]
         make_piece_tiles(1, "x_codes0")
-        round_columns(1, whole[1], nc.scalar.copy)
+        round_columns(1, slice(0, LEAD), nc.scalar.copy)
+        round_columns(1, slice(LEAD, FIRST), nc.scalar.copy)
         quantize(1, whole[1])
-        gelu(2, raw[1][:, 0, 0:FIRST], acc[2][:, 0:FIRST])
-        place(2, 0, FIRST, raw[1][:, 0, 0:FIRST])
-        finish(3, 0, FIRST, "values3a")
-        make_piece_tiles(2, "rounded2")
-        round_columns(2, slice(0, 64), nc.scalar.copy, 1, slice(128, 192))
+        for m, values in ((2, flat[1][:, 0:FIRST]), (3, raw[1][:, 1, :])):
+            gelu(m, values, acc[m][:, 0:FIRST])
+            place(m, 0, FIRST, values)
         for m in range(ROW_TILES):
             multiply_piece(m, 1)
+        finish(0, *PIECES[1], "values0b")
+        finish(1, *PIECES[1], "values1b")
 
-        round_columns(2, slice(64, 256), nc.scalar.copy, 2, slice(0, 192))
+        make_piece_tiles(2, "x_codes1")
+        round_columns(2, whole[2], nc.scalar.copy)
         quantize(2, whole[2])
-        for m in range(ROW_TILES):
-            lo, hi = PIECES[1]
+        lo, hi = PIECES[1]
+        for m in (2, 3):
             gelu(m, raw[2][:, m, 0 : hi - lo], acc[m][:, lo:hi])
             place(m, lo, hi, raw[2][:, m, 0 : hi - lo])
         for m in range(ROW_TILES):

@@ -170,6 +170,9 @@ def tile_list_hscat_gelu_kernel(tc, x, w_words, w_scales, b, wgo, offs, out):
         for m in range(ROW_TILES):
             multiply_piece(m, 2)
 
-        for m in range(ROW_TILES):
-            finish(m, *PIECES[2], f"values{m}c")
-            nc.sync.dma_start(out[P * m : P * (m + 1), :], windows[m][:])
+        lo, hi = PIECES[2]
+        mid = lo + FIRST
+        for m, begin, end in ((0, lo, mid), (1, lo, mid), (0, mid, hi), (2, lo, mid), (1, mid, hi), (2, mid, hi), (3, lo, hi)):
+            finish(m, begin, end, f"values{m}_{begin}")
+            if end == hi:
+                nc.sync.dma_start(out[P * m : P * (m + 1), :], windows[m][:])

from contextlib import ExitStack

import concourse.mybir as mybir

K, M, T, S = 512, 512, 1024, 512
FLOPS = 2 * K * M * S

F32 = mybir.dt.float32
BF16 = mybir.dt.bfloat16
I32 = mybir.dt.int32
U32 = mybir.dt.uint32
U16 = mybir.dt.uint16
U8 = mybir.dt.uint8
FP8X4 = mybir.dt.float8_e4m3fn_x4
GELU = mybir.ActivationFunctionType.Gelu_apprx_tanh
MULT = mybir.AluOpType.mult

P = 128
PACK = 4
GROUP = 16
ROW_TILES = M // P
PIECES = [(0, 128), (128, 256), (256, 512)]
LOADS = PIECES
FIRST = PIECES[0][1]
LEAD = 16
HALF = FIRST // 2


def tile_list_hscat_gelu_kernel(tc, x, w_words, w_scales, b, wgo, offs, out):
    nc = tc.nc
    with ExitStack() as ctx:
        lists = ctx.enter_context(tc.tile_pool(name="lists", bufs=1))
        keep = ctx.enter_context(tc.tile_pool(name="keep", bufs=1))
        psum = ctx.enter_context(tc.psum_pool(name="psum", bufs=1))

        offsets = lists.tile([P, S // GROUP], U16, name="offsets")
        w_codes = keep.tile([P, M], U32, name="w_codes", align_bytes=64)
        w_scale = keep.tile([P, M], U8, name="w_scale", align_bytes=64)
        bias = keep.tile([P, ROW_TILES], F32, name="bias")
        wgo_sb = keep.tile([P, S], F32, name="wgo_sb")
        room = [0, FIRST - LEAD, 0]
        flat = [
            keep.tile([P, room[h] + PACK * (hi - lo)], F32, name=f"raw{h}", tag=f"raw{h}", align_bytes=64)
            for h, (lo, hi) in enumerate(LOADS)
        ]
        raw = [flat[h][:, room[h] :].rearrange("p (t c) -> p t c", t=PACK) for h in range(len(LOADS))]
        warm = keep.tile([P, 1], F32, name="warm")

        x_rows = x.rearrange("(p t) c -> p t c", t=PACK)
        def load_scale(q, queue):
            queue.dma_start(
                w_scale[32 * q : 32 * q + 4, :].bitcast(I32), w_scales[0, 4 * q : 4 * q + 4, :].bitcast(I32)
            )

        load_scale(0, nc.scalar)
        nc.sync.dma_start(raw[0], x_rows[:, :, 0:FIRST])
        nc.vector.memset(warm[:], 0.0)
        nc.scalar.activation(warm[:], warm[:], GELU)
        for q in (1, 2, 3):
            load_scale(q, nc.sync)
        nc.sync.dma_start(w_codes[:].bitcast(I32), w_words[0].rearrange("p n t -> p (n t)").bitcast(I32))
        with nc.allow_non_contiguous_dma(reason="one bias value a partition"):
            nc.sync.dma_start(bias[:], b.rearrange("(m p) -> p m", p=P))
        nc.sync.dma_start(wgo_sb[:, 0:FIRST], wgo[:, 0:FIRST])
        nc.sync.dma_start(offsets[:], offs)
        for h in (1, 2):
            lo, hi = LOADS[h]
            nc.sync.dma_start(raw[h], x_rows[:, :, lo:hi])
        nc.sync.dma_start(wgo_sb[:, FIRST:S], wgo[:, FIRST:S])

        windows = {}

        def clear(m, engine, tag):
            windows[m] = keep.tile([P, T], F32, name=f"window{m}", tag=tag, align_bytes=64)
            engine.memset(windows[m][:].bitcast(I32), 0)

        rounded, x_codes, x_scale = {}, {}, {}

        def make_piece_tiles(h, rounded_tag):
            width = PIECES[h][1] - PIECES[h][0]
            rounded[h] = keep.tile([P, width, PACK], BF16, name=f"rounded{h}", tag=rounded_tag, align_bytes=64)
            x_codes[h] = keep.tile([P, width], U32, name=f"x_codes{h}", tag=f"x_codes{h}", align_bytes=64)
            x_scale[h] = keep.tile([P, width], U8, name=f"x_scale{h}", tag=f"x_scale{h}", align_bytes=64)

        def round_columns(h, cols, copy, load=None, load_cols=None):
            copy(
                rounded[h][:, cols, :].rearrange("p (c i) t -> p c t i", i=4),
                raw[h if load is None else load][:, :, load_cols or cols].rearrange("p t (c i) -> p c t i", i=4),
            )

        def quantize(h, cols):
            nc.vector.quantize_mx(
                out=x_codes[h][:, cols].bitcast(FP8X4),
                scales=x_scale[h][:, cols],
                in_=rounded[h][:, cols, :].rearrange("p c t -> p (c t)"),
            )

        def multiply(m, h, cols, sums):
            rows = slice(P * m, P * (m + 1))
            nc.tensor.matmul_mx(
                out=sums,
                lhsT=w_codes[:, rows].bitcast(FP8X4),
                lhsT_scale=w_scale[:, rows],
                rhs=x_codes[h][:, cols].bitcast(FP8X4),
                rhs_scale=x_scale[h][:, cols],
                start=True,
                stop=True,
            )

        def multiply_piece(m, h):
            lo, hi = PIECES[h]
            multiply(m, h, slice(0, hi - lo), acc[m][:, lo:hi])

        def gelu(m, result, sums):
            nc.scalar.activation(result, sums, GELU, bias=bias[:, m : m + 1])

        def place(m, lo, hi, values):
            listed = windows[m][:].indirect(offsets[:, lo // GROUP : hi // GROUP])
            nc.vector.tensor_tensor(listed, values, wgo_sb[:, lo:hi], MULT)

        def finish(m, lo, hi, tag):
            values = keep.tile([P, hi - lo], F32, name=f"values{m}_{lo}", tag=tag, align_bytes=64)
            gelu(m, values[:], acc[m][:, lo:hi])
            place(m, lo, hi, values[:])

        clear(0, nc.vector, "window0")
        clear(1, nc.vector, "window1")

        acc = [psum.tile([P, S], F32, name=f"acc{m}") for m in range(ROW_TILES)]

        halves = [slice(0, HALF), slice(HALF, FIRST)]
        make_piece_tiles(0, "rounded0")
        round_columns(0, halves[0], nc.vector.tensor_copy)
        round_columns(0, halves[1], nc.scalar.copy)
        lead = [psum.tile([P, HALF], F32, name=f"lead{u}") for u in range(2)]
        for cols, sums in zip(halves, lead):
            quantize(0, cols)
            multiply(0, 0, cols, sums[:])
        for m in range(1, ROW_TILES):
            multiply_piece(m, 0)
        clear(2, nc.gpsimd, "rounded0")
        clear(3, nc.gpsimd, "x_scale0")

        lead_values = keep.tile([P, FIRST], F32, name="lead_values", align_bytes=64)
        for cols, sums in zip(halves, lead):
            gelu(0, lead_values[:, cols], sums[:])
        place(0, 0, FIRST, lead_values[:])
        finish(1, 0, FIRST, "values1a")

        whole = [slice(0, hi - lo) for lo, hi in PIECES]
        make_piece_tiles(1, "x_codes0")
        round_columns(1, slice(0, LEAD), nc.scalar.copy)
        round_columns(1, slice(LEAD, FIRST), nc.scalar.copy)
        quantize(1, whole[1])
        for m, values in ((2, flat[1][:, 0:FIRST]), (3, raw[1][:, 1, :])):
            gelu(m, values, acc[m][:, 0:FIRST])
            place(m, 0, FIRST, values)
        for m in range(ROW_TILES):
            multiply_piece(m, 1)
        finish(0, *PIECES[1], "values0b")
        finish(1, *PIECES[1], "values1b")

        make_piece_tiles(2, "x_codes1")
        round_columns(2, whole[2], nc.scalar.copy)
        quantize(2, whole[2])
        lo, hi = PIECES[1]
        for m in (2, 3):
            gelu(m, raw[2][:, m, 0 : hi - lo], acc[m][:, lo:hi])
            place(m, lo, hi, raw[2][:, m, 0 : hi - lo])
        for m in range(ROW_TILES):
            multiply_piece(m, 2)

        lo, hi = PIECES[2]
        mid = lo + FIRST
        for m, begin, end in ((0, lo, mid), (1, lo, mid), (0, mid, hi), (2, lo, mid), (1, mid, hi), (2, mid, hi), (3, lo, hi)):
            finish(m, begin, end, f"values{m}_{begin}")
            if end == hi:
                nc.sync.dma_start(out[P * m : P * (m + 1), :], windows[m][:])
